import numpy as np, ml_dtypes
CORES = [10,34,74,98]
N = 4
import mx_ref
NC, KT, G, WT = 128, 1, 4, 1
C = np.float32(0.019)
BF = ml_dtypes.bfloat16
def cut(t, i, w=512):
    return t[:, w * i:w * i + w]
def tile(rs):
    return np.stack(rs, axis=2).reshape(128, -1).astype(BF)
def layer(w, X):
    out = []
    for i in range(G):
        for t in range(len(X)):
            p = mx_ref.matmul(mx_ref.quantize(cut(w, len(X) * i + t)), X[t])
            z = p if t == 0 else z + p
        out.append(z)
    return out
def act(Z):
    return [np.maximum(z, 0) * C for z in Z]
def setup_inputs(rng):
    def f(*shape):
        return mx_ref.flush((rng.standard_normal(shape, dtype=np.float32) * np.exp2(rng.integers(-2, 3, shape[:-1] + (1,)))).astype(BF))
    return {"x": f(N, 128, KT * 4 * NC), "w1": f(N, 128, G * KT * 512), "w2": f(N, 128, WT * 512)}
def setup_inputs_blocks(rng):
    d = setup_inputs(rng)
    for k in ("x", "w1", "w2"): d[k] = mx_ref.spread(d[k], rng, 4)
    return d
def setup_inputs_wide(rng):
    d = setup_inputs(rng)
    for k in ("x", "w1", "w2"): d[k] = mx_ref.flush((d[k].astype(np.float32) * np.exp2(rng.integers(-8, 9, (N, 1, 1))).astype(np.float32)).astype(BF))
    return d
def setup_inputs_zeros(rng):
    d = setup_inputs(rng); v = d["x"].reshape(N, 128, -1, 4).copy()
    v[np.broadcast_to((rng.random((N, 1, v.shape[2], 1)) < 0.33), v.shape)] = 0
    d["x"] = v.reshape(d["x"].shape)
    return d
def reference(x, w1, w2):
    H = [mx_ref.quantize(tile(act(layer(w1[j], [mx_ref.quantize(cut(x[j], t, 4 * NC)) for t in range(KT)])))) for j in range(N)]
    y = np.zeros((N, 128, N * WT * NC), np.float32)
    for r in range(N):
        for i in range(WT):
            qw = mx_ref.quantize(cut(w2[r], i))
            for j in range(N):
                y[r][:, NC * (WT * j + i):NC * (WT * j + i) + NC] = mx_ref.matmul(qw, H[j])
    return {"y": y}

import numpy as np
from concourse.bass import DstId, RemoteDMATransfer
from concourse.mybir import dt, ActivationFunctionType

N = 4
NC = 128
G = 4
C = float(np.float32(0.019))

SCRATCH = {
    "xb": ("sbuf", [128, 512], "bfloat16"),
    "w1b": ("sbuf", [128, 2048], "bfloat16"),
    "w2b": ("sbuf", [128, 512], "bfloat16"),
    "xq": ("sbuf", [128, 128], "float8_e4m3fn_x4"),
    "xs": ("sbuf", [128, 128], "uint8"),
    "w1q": ("sbuf", [128, 512], "float8_e4m3fn_x4"),
    "w1s": ("sbuf", [128, 512], "uint8"),
    "w2q": ("sbuf", [128, 128], "float8_e4m3fn_x4"),
    "w2s": ("sbuf", [128, 128], "uint8"),
    "hb": ("sbuf", [128, 512], "bfloat16"),
    "hq": ("sbuf", [128, 512], "float8_e4m3fn_x4"),
    "hs": ("sbuf", [128, 512], "uint8"),
    "z": ("psum", [128, 2048], "float32"),
    "yp": ("psum", [128, 2048], "float32"),
    "yb": ("sbuf", [128, 512], "float32"),
}
SEMAPHORES = ["ldx", "ldw1a", "ldw1b", "ldw2", "qx", "qw2", "qh", "act", "sent", "st",
              "qw1t0", "qw1t1", "qw1t2", "qw1t3", "mm0", "mm1", "mm2", "mm3", "arr0", "arr1", "arr2", "arr3",
              "ymm0", "ymm1", "ymm2", "ymm3", "ycp0", "ycp1", "ycp2", "ycp3"]


def rank_program(g, core, T, topo):
    rank = T.rank_of(core)
    if rank is None:
        return
    S = T.sem
    cores = T.cores
    v, t, a, sy = g.vector, g.tensor, g.scalar, g.sync

    def slot(i):
        return slice(NC * i, NC * i + NC)

    ks = sorted(range(1, N), key=lambda k: (topo.same_plane(topo.chip(core), topo.chip(cores[rank ^ k])), k))
    peers = [rank ^ k for k in ks]

    head = (G - 1) * 512
    sy.dma_start(T.xb[:], T.x[:]).then_inc(S.ldx, 16)
    a.dma_start(T.w1b[:, 0:head], T.w1[:, 0:head]).then_inc(S.ldw1a, 16)
    sy.dma_start(T.w1b[:, head:], T.w1[:, head:]).then_inc(S.ldw1b, 16)
    sy.dma_start(T.w2b[:], T.w2[:]).then_inc(S.ldw2, 16)

    v.wait_ge(S.ldx, 16)
    v.quantize_mx(T.xq[:], T.xs[:], T.xb[:]).then_inc(S.qx, 1)
    v.wait_ge(S.ldw1a, 16)
    for i in range(G):
        if i == G - 1:
            v.wait_ge(S.ldw1b, 16)
        v.quantize_mx(T.w1q[:, slot(i)], T.w1s[:, slot(i)], T.w1b[:, 512 * i:512 * i + 512]).then_inc(S["qw1t%d" % i], 1)
    t.wait_ge(S.qx, 1)
    for i in range(G):
        t.wait_ge(S["qw1t%d" % i], 1)
        t.matmul_mx(T.z[:, 512 * i:512 * i + NC], T.w1q[:, slot(i)], T.w1s[:, slot(i)], T.xq[:], T.xs[:],
                    True, True).then_inc(S["mm%d" % i], 1)
        a.wait_ge(S["mm%d" % i], 1)
        a.activation(T.hb[:, i:4 * NC:4], T.z[:, 512 * i:512 * i + NC], ActivationFunctionType.Relu,
                     scale=C).then_inc(S.act, 1)
    v.wait_ge(S.act, G)
    v.quantize_mx(T.hq[:, slot(rank)], T.hs[:, slot(rank)], T.hb[:]).then_inc(S.qh, 1)
    v.wait_ge(S.ldw2, 16)
    v.quantize_mx(T.w2q[:], T.w2s[:], T.w2b[:]).then_inc(S.qw2, 1)

    mask = topo.mask(core, cores[peers[0]])
    for p in peers:
        mask &= topo.mask(core, cores[p])
    eng = bin(mask).count("1")
    arrive = S["arr%d" % rank]
    g.wait_ge(S.qh, 1)
    g.remote_dma_fused([RemoteDMATransfer(
        dst_ids=[DstId(rid=topo.addr(cores[p])[0], pnc=topo.addr(cores[p])[1]) for p in peers],
        dma_engine_mask=mask, remote_sem=arrive,
        srcs=[T.hs[:, slot(rank)]], dsts=[T.hs[:, slot(rank)] for p in peers])], local_sem=S.sent)
    for p in peers:
        rid, pid, _ = topo.addr(cores[p])
        g.remote_dma(T.hq[:, slot(rank)].bitcast(dt.uint8), T.hq[:, slot(rank)].bitcast(dt.uint8),
                     arrive, S.sent, pid, rid, mask)

    def block(i):
        t.matmul_mx(T.yp[:, 512 * i:512 * i + NC], T.w2q[:], T.w2s[:], T.hq[:, slot(i)], T.hs[:, slot(i)],
                    True, True).then_inc(S["ymm%d" % i], 1)
        v.wait_ge(S["ymm%d" % i], 1)
        v.tensor_copy(T.yb[:, slot(i)], T.yp[:, 512 * i:512 * i + NC]).then_inc(S["ycp%d" % i], 1)

    t.wait_ge(S.qh, 1)
    t.wait_ge(S.qw2, 1)
    block(rank)
    for p in peers:
        t.wait_ge(S["arr%d" % p], 2 * eng)
        block(p)

    stores = 0
    groups = [[rank, peers[0]]] if abs(rank - peers[0]) == 1 else [[rank], [peers[0]]]
    groups += [[p] for p in peers[1:]]
    for grp in groups:
        for i in grp:
            sy.wait_ge(S["ycp%d" % i], 1)
        lo, hi = NC * min(grp), NC * max(grp) + NC
        sy.dma_start(T.y[:, lo:hi], T.yb[:, lo:hi]).then_inc(S.st, 16)
        stores += 1
    sy.wait_ge(S.st, 16 * stores)
    g.wait_ge(S.sent, (1 + len(peers)) * eng)
